import numpy as np
import ml_dtypes


def mxq(x, axis, fmt="e4m3"):
    dtype, down = {"e4m3": (ml_dtypes.float8_e4m3fn, 7), "e5m2": (ml_dtypes.float8_e5m2, 14)}[fmt]
    v = np.moveaxis(np.asarray(x, np.float32).astype(ml_dtypes.bfloat16).astype(np.float64), axis, -1)
    blocks = v.reshape(v.shape[:-1] + (-1, 32))
    amax = np.abs(blocks).max(-1, keepdims=True)
    byte = np.maximum(np.where(amax > 0, np.frexp(amax)[1] - 1 + 127, 0) - down, 1)
    scale = np.exp2(byte - 127.0)
    codes = (blocks / scale).astype(np.float32).astype(dtype).astype(np.float64)
    return np.moveaxis((codes * scale).reshape(v.shape), -1, axis)


WIDE = False


def mx_kscale(k):
    if not WIDE:
        return np.ones(k)
    levels = np.array([10, -10, 5, -5, 0])
    if k % 512:
        return np.exp2(np.random.permutation(np.resize(levels, k // 32))).repeat(32)
    a = np.empty((k // 512, 16))
    for p in range(k // 512):
        a[p, :8] = np.random.permutation(np.resize(levels, 8))
        for g in range(8):
            far = levels[np.abs(levels - a[p, g]) >= 10]
            a[p, g + 8] = far[np.random.randint(len(far))]
    return np.exp2(a.ravel()).repeat(32)


def f64(x):
    return np.asarray(x).astype(np.float64)


def striped8(idx):
    return np.concatenate([v.reshape(-1, 16).T for v in idx]).astype(np.uint16)


def unstriped8(offs):
    return np.stack([offs[16 * g:16 * g + 16].T.reshape(-1) for g in range(8)]).astype(np.int64)


E2M1 = np.array([0.0, 0.5, 1.0, 1.5, 2.0, 3.0, 4.0, 6.0, -0.0, -0.5, -1.0, -1.5, -2.0, -3.0, -4.0, -6.0])


def pack_weight(w, fmt):
    k, n = w.shape
    w = f64(np.asarray(w, np.float32).astype(ml_dtypes.bfloat16)).reshape(k // 32, 32, n)
    amax = np.abs(w).max(1)
    if fmt == "e4m3":
        byte = np.frexp(amax)[1] - 1 + 127 - 7
    else:
        mant, ex = np.frexp(amax / 6.0)
        byte = np.where(mant > 0.5, ex, ex - 1) + 127
    byte = np.clip(np.where(amax > 0, byte, 1), 1, 254)
    scaled = (w * np.exp2(127.0 - byte)[:, None, :]).reshape(k, n).astype(np.float32)
    by_word = np.ascontiguousarray(scaled.reshape(k // 512, 128, 4, n).transpose(0, 1, 3, 2))
    if fmt == "e4m3":
        words = by_word.astype(ml_dtypes.float8_e4m3fn).view(np.uint8)
    else:
        c = by_word.astype(ml_dtypes.float4_e2m1fn).view(np.uint8) & 0xF
        words = (c[..., 0::2] | (c[..., 1::2] << 4)).reshape(k // 512, 128, 2 * n)
    return np.ascontiguousarray(words), np.ascontiguousarray(byte.astype(np.uint8).reshape(k // 512, 16, n))


def unpack_weight(words, scales, fmt):
    g, _, n = scales.shape
    words = np.ascontiguousarray(words).reshape(g, 128, n, -1)
    if fmt == "e4m3":
        vals = words.view(ml_dtypes.float8_e4m3fn).astype(np.float64)
    else:
        nib = np.empty((g, 128, n, 4), np.uint8)
        nib[..., 0::2] = words & 0xF
        nib[..., 1::2] = words >> 4
        vals = E2M1[nib]
    vals = vals * np.repeat(np.exp2(scales.astype(np.float64) - 127.0), 8, axis=1)[..., None]
    return vals.transpose(0, 1, 3, 2).reshape(g * 512, n)


K, L, M, T, S = 1024, 512, 128, 2048, 1024


def setup_inputs():
    n = np.random.standard_normal
    s1 = mx_kscale(K)[:, None]
    s2 = mx_kscale(L)[:, None]
    p_w4 = pack_weight(n((K, M)) / np.sqrt(K) / s1, "e2m1")
    return {
        "xT": (n((K, T)) * s1).astype(np.float32),
        "w4_words": p_w4[0],
        "w4_scales": p_w4[1],
        "c": (n((L, S)) * s2).astype(np.float32),
        "u": (n((L, M)) / np.sqrt(L) / s2).astype(np.float32),
        "wgt": np.repeat(np.random.uniform(0.5, 2.0, (8, S)), 16, axis=0).astype(np.float32),
        "offs": striped8(np.stack([np.random.permutation(T)[:S] for _ in range(8)])),
    }


def reference(xT, w4_words, w4_scales, c, u, wgt, offs):
    idx = unstriped8(offs)
    group = np.arange(K) % 512 // 64
    xg = f64(wgt)[np.arange(K) // 4 % 128] * f64(xT)[np.arange(K)[:, None], idx[group]]
    xT_ = mxq(xg, 0, "e4m3")
    w4_ = unpack_weight(w4_words, w4_scales, "e2m1")
    c_ = mxq(f64(c), 0, "e4m3")
    u_ = mxq(f64(u), 0, "e4m3")
    y = xT_.T @ w4_ + c_.T @ u_
    return y

@@ -1,0 +1,165 @@
+from contextlib import ExitStack
+
+import concourse.mybir as mybir
+
+K, L, M, T, S = 1024, 512, 128, 2048, 1024
+FLOPS = 2 * (K + L) * M * S
+
+F32 = mybir.dt.float32
+BF16 = mybir.dt.bfloat16
+U32 = mybir.dt.uint32
+I32 = mybir.dt.int32
+U16 = mybir.dt.uint16
+U8 = mybir.dt.uint8
+FP8X4 = mybir.dt.float8_e4m3fn_x4
+FP4X4 = mybir.dt.float4_e2m1fn_x4
+
+P = 128
+PACK = 4
+H = 512
+
+
+def tile_list_hmix_tm_none_kernel(tc, xT, w4_words, w4_scales, c, u, wgt, offs, out):
+    nc = tc.nc
+    mult = mybir.AluOpType.mult
+    with ExitStack() as ctx:
+        keep = ctx.enter_context(tc.tile_pool(name="keep", bufs=1))
+        psum = ctx.enter_context(tc.psum_pool(name="psum", bufs=1))
+
+        offsets = keep.tile([P, S // 16], U16, name="offsets")
+        nc.sync.dma_start(offsets[:], offs)
+
+        w4w = keep.tile([P, 2, 2 * M], U8, name="w4w", align_bytes=64)
+        w4s = keep.tile([P, 2, M], U8, name="w4s", align_bytes=64)
+        nc.gpsimd.memset(w4s[:].bitcast(I32), 0)
+        nc.scalar.dma_start(w4w[:].bitcast(I32), w4_words.bitcast(I32).rearrange("a p n -> p a n"))
+        for q in range(4):
+            nc.scalar.dma_start(
+                w4s[32 * q : 32 * q + 4, :, :].bitcast(I32),
+                w4_scales.bitcast(I32)[:, 4 * q : 4 * q + 4, :].rearrange("a r n -> r a n"),
+            )
+
+        planes_hbm = xT.rearrange("(a p i) t -> a i p t", a=2, i=PACK)
+        planes = {}
+        wg = {}
+
+        def load_plane(a, i):
+            planes[a, i] = keep.tile([P, T], F32, name=f"plane{a}{i}")
+            nc.sync.dma_start(planes[a, i][:], planes_hbm[a, i])
+
+        load_plane(0, 0)
+        for h in range(2):
+            wg[h] = keep.tile([P, H], F32, name=f"wgt{h}")
+            nc.sync.dma_start(wg[h][:], wgt[:, h * H : (h + 1) * H])
+        for a, i in ((0, 1), (0, 2), (0, 3), (1, 0), (1, 1), (1, 2), (1, 3)):
+            load_plane(a, i)
+        u_raw = keep.tile([P, PACK, M], F32, name="u_raw")
+        nc.sync.dma_start(u_raw[:], u.rearrange("(p i) n -> p i n", i=PACK))
+        c_hbm = c.rearrange("(p i) j -> p i j", i=PACK)
+        c_cuts = ((0, 512), (512, 256), (768, 256))
+        c_raw = []
+        for j0, w in c_cuts:
+            raw = keep.tile([P, PACK, w], F32, name=f"c_raw{j0}")
+            nc.sync.dma_start(raw[:], c_hbm[:, :, j0 : j0 + w])
+            c_raw.append(raw)
+
+        def interleave(engine_copy, dst, src, w, i0, i1):
+            engine_copy(
+                dst[:].rearrange("p (j i) -> p i j", i=PACK)[:, i0:i1, :].rearrange("p i (g e) -> p g i e", e=4),
+                src[:][:, i0:i1, :].rearrange("p i (g e) -> p g i e", e=4),
+            )
+
+        def quantize(name, src, w):
+            codes = keep.tile([P, w], U32, name=f"codes_{name}", align_bytes=64)
+            scales = keep.tile([P, w], U8, name=f"scales_{name}", align_bytes=64)
+            nc.vector.quantize_mx(out=codes[:].bitcast(FP8X4), scales=scales[:], in_=src[:])
+            return codes, scales
+
+        picked = {}
+        packed = {}
+        for a in range(2):
+            for h in range(2):
+                picked[a, h] = keep.tile([P, PACK, H], F32, name=f"picked{a}{h}")
+                packed[a, h] = keep.tile([P, H * PACK], BF16, name=f"packed{a}{h}", align_bytes=64)
+
+        def gather(a, i, h):
+            k0 = h * (H // 16)
+            nc.vector.tensor_tensor(
+                picked[a, h][:, i, :],
+                planes[a, i][:].indirect(offsets[:, k0 : k0 + H // 16]),
+                wg[h][:],
+                mult,
+            )
+
+        xq = {}
+        for i in range(PACK):
+            gather(0, i, 0)
+            gather(0, i, 1)
+        for h in range(2):
+            interleave(nc.scalar.copy, packed[0, h], picked[0, h], H, 0, 4)
+        for i in range(2):
+            gather(1, i, 0)
+            gather(1, i, 1)
+        for h in range(2):
+            interleave(nc.scalar.copy, packed[1, h], picked[1, h], H, 0, 2)
+        u_packed = keep.tile([P, M * PACK], BF16, name="u_packed", align_bytes=64)
+        interleave(nc.scalar.copy, u_packed, u_raw, M, 0, 4)
+        for i in range(2, PACK):
+            gather(1, i, 0)
+            gather(1, i, 1)
+        uq = quantize("u", u_packed, M)
+        for h in range(2):
+            interleave(nc.scalar.copy, packed[1, h], picked[1, h], H, 2, 4)
+
+        c_packed = []
+        for j0, w in c_cuts:
+            c_packed.append(keep.tile([P, w * PACK], BF16, name=f"c_packed{j0}", align_bytes=64))
+        cq = [None, None, None]
+        xq[0, 0] = quantize("x00", packed[0, 0], H)
+        interleave(nc.vector.tensor_copy, c_packed[0], c_raw[0], 512, 0, 4)
+        xq[1, 0] = quantize("x10", packed[1, 0], H)
+        cq[0] = quantize("c0", c_packed[0], 512)
+        interleave(nc.scalar.copy, c_packed[1], c_raw[1], 256, 0, 4)
+        xq[0, 1] = quantize("x01", packed[0, 1], H)
+        xq[1, 1] = quantize("x11", packed[1, 1], H)
+        interleave(nc.scalar.copy, c_packed[2], c_raw[2], 256, 0, 4)
+        cq[1] = quantize("c1", c_packed[1], 256)
+        cq[2] = quantize("c2", c_packed[2], 256)
+
+        c_at = {}
+        for t in range(8):
+            c_at[t] = (0, 128 * t) if t < 4 else (1, 128 * (t - 4)) if t < 6 else (2, 128 * (t - 6))
+        banks = {}
+        for t in range(8):
+            banks[t] = psum.tile([P, M], F32, name=f"bank{t}")
+            h, o = divmod(t, 4)
+            cols = slice(o * P, (o + 1) * P)
+            for a in range(2):
+                codes, scales = xq[a, h]
+                nc.tensor.matmul_mx(
+                    out=banks[t][:],
+                    lhsT=codes[:, cols].bitcast(FP8X4),
+                    lhsT_scale=scales[:, cols],
+                    rhs=w4w[:, a, :].bitcast(FP4X4),
+                    rhs_scale=w4s[:, a, :],
+                    start=(a == 0),
+                    stop=False,
+                )
+            b, o = c_at[t]
+            codes, scales = cq[b]
+            cols = slice(o, o + P)
+            nc.tensor.matmul_mx(
+                out=banks[t][:],
+                lhsT=codes[:, cols].bitcast(FP8X4),
+                lhsT_scale=scales[:, cols],
+                rhs=uq[0][:].bitcast(FP8X4),
+                rhs_scale=uq[1][:],
+                start=False,
+                stop=True,
+            )
+        out_hbm = out.rearrange("(r t p) n -> r p t n", t=2, p=P)
+        for r in range(4):
+            res = keep.tile([P, 2, M], F32, name=f"res{r}")
+            nc.scalar.copy(res[:, 0, :], banks[2 * r][:])
+            nc.vector.tensor_copy(res[:, 1, :], banks[2 * r + 1][:])
+            nc.sync.dma_start(out_hbm[r], res[:])

@@ -32,12 +32,6 @@ def tile_list_hmix_tm_none_kernel(tc, xT, w4_words, w4_scales, c, u, wgt, offs, 
         w4w = keep.tile([P, 2, 2 * M], U8, name="w4w", align_bytes=64)
         w4s = keep.tile([P, 2, M], U8, name="w4s", align_bytes=64)
         nc.gpsimd.memset(w4s[:].bitcast(I32), 0)
-        nc.scalar.dma_start(w4w[:].bitcast(I32), w4_words.bitcast(I32).rearrange("a p n -> p a n"))
-        for q in range(4):
-            nc.scalar.dma_start(
-                w4s[32 * q : 32 * q + 4, :, :].bitcast(I32),
-                w4_scales.bitcast(I32)[:, 4 * q : 4 * q + 4, :].rearrange("a r n -> r a n"),
-            )
 
         planes_hbm = xT.rearrange("(a p i) t -> a i p t", a=2, i=PACK)
         planes = {}
@@ -47,32 +41,43 @@ def tile_list_hmix_tm_none_kernel(tc, xT, w4_words, w4_scales, c, u, wgt, offs, 
             planes[a, i] = keep.tile([P, T], F32, name=f"plane{a}{i}")
             nc.sync.dma_start(planes[a, i][:], planes_hbm[a, i])
 
+        c_hbm = c.rearrange("(p i) j -> p i j", i=PACK)
+        c_raw = {}
+
+        def load_c(j0, w):
+            c_raw[j0] = keep.tile([P, PACK, w], F32, name=f"c_raw{j0}")
+            nc.sync.dma_start(c_raw[j0][:], c_hbm[:, :, j0 : j0 + w])
+
         load_plane(0, 0)
         for h in range(2):
             wg[h] = keep.tile([P, H], F32, name=f"wgt{h}")
             nc.sync.dma_start(wg[h][:], wgt[:, h * H : (h + 1) * H])
-        for a, i in ((0, 1), (0, 2), (0, 3), (1, 0), (1, 1), (1, 2), (1, 3)):
+        for a, i in ((0, 1), (0, 2), (0, 3), (1, 0), (1, 1)):
             load_plane(a, i)
         u_raw = keep.tile([P, PACK, M], F32, name="u_raw")
         nc.sync.dma_start(u_raw[:], u.rearrange("(p i) n -> p i n", i=PACK))
-        c_hbm = c.rearrange("(p i) j -> p i j", i=PACK)
-        c_cuts = ((0, 512), (512, 256), (768, 256))
-        c_raw = []
-        for j0, w in c_cuts:
-            raw = keep.tile([P, PACK, w], F32, name=f"c_raw{j0}")
-            nc.sync.dma_start(raw[:], c_hbm[:, :, j0 : j0 + w])
-            c_raw.append(raw)
+        load_plane(1, 2)
+        load_c(0, 256)
+        load_plane(1, 3)
+        for j0 in (256, 512, 768):
+            load_c(j0, 256)
+        nc.scalar.dma_start(w4w[:].bitcast(I32), w4_words.bitcast(I32).rearrange("a p n -> p a n"))
+        for q in range(4):
+            nc.scalar.dma_start(
+                w4s[32 * q : 32 * q + 4, :, :].bitcast(I32),
+                w4_scales.bitcast(I32)[:, 4 * q : 4 * q + 4, :].rearrange("a r n -> r a n"),
+            )
 
-        def interleave(engine_copy, dst, src, w, i0, i1):
+        def interleave(engine_copy, dst, src):
             engine_copy(
-                dst[:].rearrange("p (j i) -> p i j", i=PACK)[:, i0:i1, :].rearrange("p i (g e) -> p g i e", e=4),
-                src[:][:, i0:i1, :].rearrange("p i (g e) -> p g i e", e=4),
+                dst.rearrange("p (g e i) -> p g i e", i=PACK, e=4),
+                src.rearrange("p i (g e) -> p g i e", e=4),
             )
 
         def quantize(name, src, w):
             codes = keep.tile([P, w], U32, name=f"codes_{name}", align_bytes=64)
             scales = keep.tile([P, w], U8, name=f"scales_{name}", align_bytes=64)
-            nc.vector.quantize_mx(out=codes[:].bitcast(FP8X4), scales=scales[:], in_=src[:])
+            nc.vector.quantize_mx(out=codes[:].bitcast(FP8X4), scales=scales[:], in_=src)
             return codes, scales
 
         picked = {}
@@ -82,49 +87,54 @@ def tile_list_hmix_tm_none_kernel(tc, xT, w4_words, w4_scales, c, u, wgt, offs, 
                 picked[a, h] = keep.tile([P, PACK, H], F32, name=f"picked{a}{h}")
                 packed[a, h] = keep.tile([P, H * PACK], BF16, name=f"packed{a}{h}", align_bytes=64)
 
-        def gather(a, i, h):
-            k0 = h * (H // 16)
+        def gather(a, i, h, j0=0, w=H):
+            k0 = (h * H + j0) // 16
             nc.vector.tensor_tensor(
-                picked[a, h][:, i, :],
-                planes[a, i][:].indirect(offsets[:, k0 : k0 + H // 16]),
-                wg[h][:],
+                picked[a, h][:, i, j0 : j0 + w],
+                planes[a, i][:].indirect(offsets[:, k0 : k0 + w // 16]),
+                wg[h][:, j0 : j0 + w],
                 mult,
             )
 
+        def inter_x(engine_copy, a, h, j0, w):
+            interleave(engine_copy, packed[a, h][:, j0 * 4 : (j0 + w) * 4], picked[a, h][:, :, j0 : j0 + w])
+
+        act, dve = nc.scalar.copy, nc.vector.tensor_copy
         xq = {}
+        cq = {}
+        c_packed = {}
+        for j0, w in ((0, 512), (512, 256), (768, 256)):
+            c_packed[j0] = keep.tile([P, w * PACK], BF16, name=f"c_packed{j0}", align_bytes=64)
+        u_packed = keep.tile([P, M * PACK], BF16, name="u_packed", align_bytes=64)
+
         for i in range(PACK):
             gather(0, i, 0)
             gather(0, i, 1)
-        for h in range(2):
-            interleave(nc.scalar.copy, packed[0, h], picked[0, h], H, 0, 4)
-        for i in range(2):
+        inter_x(act, 0, 0, 0, H)
+        inter_x(act, 0, 1, 0, H)
+        for i in range(3):
             gather(1, i, 0)
             gather(1, i, 1)
-        for h in range(2):
-            interleave(nc.scalar.copy, packed[1, h], picked[1, h], H, 0, 2)
-        u_packed = keep.tile([P, M * PACK], BF16, name="u_packed", align_bytes=64)
-        interleave(nc.scalar.copy, u_packed, u_raw, M, 0, 4)
-        for i in range(2, PACK):
-            gather(1, i, 0)
-            gather(1, i, 1)
-        uq = quantize("u", u_packed, M)
-        for h in range(2):
-            interleave(nc.scalar.copy, packed[1, h], picked[1, h], H, 2, 4)
-
-        c_packed = []
-        for j0, w in c_cuts:
-            c_packed.append(keep.tile([P, w * PACK], BF16, name=f"c_packed{j0}", align_bytes=64))
-        cq = [None, None, None]
-        xq[0, 0] = quantize("x00", packed[0, 0], H)
-        interleave(nc.vector.tensor_copy, c_packed[0], c_raw[0], 512, 0, 4)
-        xq[1, 0] = quantize("x10", packed[1, 0], H)
-        cq[0] = quantize("c0", c_packed[0], 512)
-        interleave(nc.scalar.copy, c_packed[1], c_raw[1], 256, 0, 4)
-        xq[0, 1] = quantize("x01", packed[0, 1], H)
-        xq[1, 1] = quantize("x11", packed[1, 1], H)
-        interleave(nc.scalar.copy, c_packed[2], c_raw[2], 256, 0, 4)
-        cq[1] = quantize("c1", c_packed[1], 256)
-        cq[2] = quantize("c2", c_packed[2], 256)
+        interleave(act, u_packed[:], u_raw[:])
+        xq[0, 0] = quantize("x00", packed[0, 0][:], H)
+        xq[0, 1] = quantize("x01", packed[0, 1][:], H)
+        interleave(act, c_packed[0][:, 0:1024], c_raw[0][:])
+        gather(1, 3, 1, 256, 256)
+        inter_x(act, 1, 1, 256, 256)
+        gather(1, 3, 1, 0, 256)
+        inter_x(act, 1, 1, 0, 256)
+        gather(1, 3, 0)
+        inter_x(act, 1, 0, 256, 256)
+        uq = quantize("u", u_packed[:], M)
+        interleave(act, c_packed[0][:, 1024:2048], c_raw[256][:])
+        inter_x(dve, 1, 0, 0, 256)
+        xq[1, 1] = quantize("x11", packed[1, 1][:], H)
+        interleave(dve, c_packed[512][:], c_raw[512][:])
+        interleave(act, c_packed[768][:], c_raw[768][:])
+        xq[1, 0] = quantize("x10", packed[1, 0][:], H)
+        cq[0] = quantize("c0", c_packed[0][:], 512)
+        cq[1] = quantize("c1", c_packed[512][:], 256)
+        cq[2] = quantize("c2", c_packed[768][:], 256)
 
         c_at = {}
         for t in range(8):

@@ -52,21 +52,21 @@ def tile_list_hmix_tm_none_kernel(tc, xT, w4_words, w4_scales, c, u, wgt, offs, 
         for h in range(2):
             wg[h] = keep.tile([P, H], F32, name=f"wgt{h}")
             nc.sync.dma_start(wg[h][:], wgt[:, h * H : (h + 1) * H])
-        for a, i in ((0, 1), (0, 2), (0, 3), (1, 0), (1, 1)):
-            load_plane(a, i)
-        u_raw = keep.tile([P, PACK, M], F32, name="u_raw")
-        nc.sync.dma_start(u_raw[:], u.rearrange("(p i) n -> p i n", i=PACK))
-        load_plane(1, 2)
-        load_c(0, 256)
-        load_plane(1, 3)
-        for j0 in (256, 512, 768):
-            load_c(j0, 256)
-        nc.scalar.dma_start(w4w[:].bitcast(I32), w4_words.bitcast(I32).rearrange("a p n -> p a n"))
+        load_plane(0, 1)
+        load_plane(0, 2)
+        nc.sync.dma_start(w4w[:].bitcast(I32), w4_words.bitcast(I32).rearrange("a p n -> p a n"))
         for q in range(4):
-            nc.scalar.dma_start(
+            nc.sync.dma_start(
                 w4s[32 * q : 32 * q + 4, :, :].bitcast(I32),
                 w4_scales.bitcast(I32)[:, 4 * q : 4 * q + 4, :].rearrange("a r n -> r a n"),
             )
+        for a, i in ((0, 3), (1, 0), (1, 1), (1, 2)):
+            load_plane(a, i)
+        u_raw = keep.tile([P, PACK, M], F32, name="u_raw")
+        nc.sync.dma_start(u_raw[:], u.rearrange("(p i) n -> p i n", i=PACK))
+        load_c(0, 512)
+        load_plane(1, 3)
+        load_c(512, 512)
 
         def interleave(engine_copy, dst, src):
             engine_copy(
@@ -103,7 +103,7 @@ def tile_list_hmix_tm_none_kernel(tc, xT, w4_words, w4_scales, c, u, wgt, offs, 
         xq = {}
         cq = {}
         c_packed = {}
-        for j0, w in ((0, 512), (512, 256), (768, 256)):
+        for j0, w in ((0, 512), (512, 512)):
             c_packed[j0] = keep.tile([P, w * PACK], BF16, name=f"c_packed{j0}", align_bytes=64)
         u_packed = keep.tile([P, M * PACK], BF16, name="u_packed", align_bytes=64)
 
@@ -116,29 +116,25 @@ def tile_list_hmix_tm_none_kernel(tc, xT, w4_words, w4_scales, c, u, wgt, offs, 
             gather(1, i, 0)
             gather(1, i, 1)
         interleave(act, u_packed[:], u_raw[:])
+        interleave(act, c_packed[0][:], c_raw[0][:])
         xq[0, 0] = quantize("x00", packed[0, 0][:], H)
         xq[0, 1] = quantize("x01", packed[0, 1][:], H)
-        interleave(act, c_packed[0][:, 0:1024], c_raw[0][:])
-        gather(1, 3, 1, 256, 256)
-        inter_x(act, 1, 1, 256, 256)
-        gather(1, 3, 1, 0, 256)
-        inter_x(act, 1, 1, 0, 256)
-        gather(1, 3, 0)
-        inter_x(act, 1, 0, 256, 256)
         uq = quantize("u", u_packed[:], M)
-        interleave(act, c_packed[0][:, 1024:2048], c_raw[256][:])
-        inter_x(dve, 1, 0, 0, 256)
-        xq[1, 1] = quantize("x11", packed[1, 1][:], H)
-        interleave(dve, c_packed[512][:], c_raw[512][:])
-        interleave(act, c_packed[768][:], c_raw[768][:])
-        xq[1, 0] = quantize("x10", packed[1, 0][:], H)
+        gather(1, 3, 0, 0, 256)
+        inter_x(act, 1, 0, 0, 256)
+        gather(1, 3, 0, 256, 256)
+        inter_x(act, 1, 0, 256, 256)
+        gather(1, 3, 1)
+        inter_x(act, 1, 1, 0, 256)
         cq[0] = quantize("c0", c_packed[0][:], 512)
-        cq[1] = quantize("c1", c_packed[512][:], 256)
-        cq[2] = quantize("c2", c_packed[768][:], 256)
+        inter_x(dve, 1, 1, 256, 256)
+        xq[1, 0] = quantize("x10", packed[1, 0][:], H)
+        xq[1, 1] = quantize("x11", packed[1, 1][:], H)
+        interleave(dve, c_packed[512][:, 0:1024], c_raw[512][:, :, 0:256])
+        interleave(act, c_packed[512][:, 1024:2048], c_raw[512][:, :, 256:512])
+        cq[1] = quantize("c1", c_packed[512][:], 512)
 
-        c_at = {}
-        for t in range(8):
-            c_at[t] = (0, 128 * t) if t < 4 else (1, 128 * (t - 4)) if t < 6 else (2, 128 * (t - 6))
+        c_at = {t: divmod(128 * t, 512) for t in range(8)}
         banks = {}
         for t in range(8):
             banks[t] = psum.tile([P, M], F32, name=f"bank{t}")

@@ -16,26 +16,30 @@ FP4X4 = mybir.dt.float4_e2m1fn_x4
 
 P = 128
 PACK = 4
-H = 512
+PASSES = K // (P * PACK)
+LISTED = 16
+HALF = S // 2
+QUARTER = S // 4
+TILES = S // P
+QUADRANT = 32
+SCALE_ROWS = 4
 
 
 def tile_list_hmix_tm_none_kernel(tc, xT, w4_words, w4_scales, c, u, wgt, offs, out):
     nc = tc.nc
-    mult = mybir.AluOpType.mult
     with ExitStack() as ctx:
         keep = ctx.enter_context(tc.tile_pool(name="keep", bufs=1))
         psum = ctx.enter_context(tc.psum_pool(name="psum", bufs=1))
 
-        offsets = keep.tile([P, S // 16], U16, name="offsets")
+        offsets = keep.tile([P, S // LISTED], U16, name="offsets")
         nc.sync.dma_start(offsets[:], offs)
 
-        w4w = keep.tile([P, 2, 2 * M], U8, name="w4w", align_bytes=64)
-        w4s = keep.tile([P, 2, M], U8, name="w4s", align_bytes=64)
-        nc.gpsimd.memset(w4s[:].bitcast(I32), 0)
+        w4_w = keep.tile([P, PASSES, 2 * M], U8, name="w4_w", align_bytes=64)
+        w4_s = keep.tile([P, PASSES, M], U8, name="w4_s", align_bytes=64)
+        nc.gpsimd.memset(w4_s[:].bitcast(I32), 0)
 
-        planes_hbm = xT.rearrange("(a p i) t -> a i p t", a=2, i=PACK)
+        planes_hbm = xT.rearrange("(a p i) t -> a i p t", a=PASSES, i=PACK)
         planes = {}
-        wg = {}
 
         def load_plane(a, i):
             planes[a, i] = keep.tile([P, T], F32, name=f"plane{a}{i}")
@@ -44,128 +48,147 @@ def tile_list_hmix_tm_none_kernel(tc, xT, w4_words, w4_scales, c, u, wgt, offs, 
         c_hbm = c.rearrange("(p i) j -> p i j", i=PACK)
         c_raw = {}
 
-        def load_c(j0, w):
-            c_raw[j0] = keep.tile([P, PACK, w], F32, name=f"c_raw{j0}")
-            nc.sync.dma_start(c_raw[j0][:], c_hbm[:, :, j0 : j0 + w])
+        def load_c(j0, width):
+            c_raw[j0] = keep.tile([P, PACK, width], F32, name=f"c_raw{j0}")
+            nc.sync.dma_start(c_raw[j0][:], c_hbm[:, :, j0 : j0 + width])
 
         load_plane(0, 0)
-        for h in range(2):
-            wg[h] = keep.tile([P, H], F32, name=f"wgt{h}")
-            nc.sync.dma_start(wg[h][:], wgt[:, h * H : (h + 1) * H])
+        weights = {}
+        for half in range(2):
+            weights[half] = keep.tile([P, HALF], F32, name=f"wgt{half}")
+            nc.sync.dma_start(weights[half][:], wgt[:, half * HALF : (half + 1) * HALF])
         load_plane(0, 1)
         load_plane(0, 2)
-        nc.sync.dma_start(w4w[:].bitcast(I32), w4_words.bitcast(I32).rearrange("a p n -> p a n"))
-        for q in range(4):
+        nc.sync.dma_start(w4_w[:].bitcast(I32), w4_words.bitcast(I32).rearrange("a p n -> p a n"))
+        for q in range(P // QUADRANT):
             nc.sync.dma_start(
-                w4s[32 * q : 32 * q + 4, :, :].bitcast(I32),
-                w4_scales.bitcast(I32)[:, 4 * q : 4 * q + 4, :].rearrange("a r n -> r a n"),
+                w4_s[QUADRANT * q : QUADRANT * q + SCALE_ROWS, :, :].bitcast(I32),
+                w4_scales.bitcast(I32)[:, SCALE_ROWS * q : SCALE_ROWS * (q + 1), :].rearrange("a r n -> r a n"),
             )
-        for a, i in ((0, 3), (1, 0), (1, 1), (1, 2)):
-            load_plane(a, i)
+        load_plane(0, 3)
+        load_plane(1, 0)
+        load_plane(1, 1)
         u_raw = keep.tile([P, PACK, M], F32, name="u_raw")
         nc.sync.dma_start(u_raw[:], u.rearrange("(p i) n -> p i n", i=PACK))
-        load_c(0, 512)
+        load_c(0, QUARTER)
+        load_plane(1, 2)
+        load_c(QUARTER, QUARTER)
         load_plane(1, 3)
-        load_c(512, 512)
+        load_c(HALF, HALF)
 
-        def interleave(engine_copy, dst, src):
+        def interleave(engine_copy, packed, raw):
             engine_copy(
-                dst.rearrange("p (g e i) -> p g i e", i=PACK, e=4),
-                src.rearrange("p i (g e) -> p g i e", e=4),
+                packed.rearrange("p (g e i) -> p g i e", i=PACK, e=4),
+                raw.rearrange("p i (g e) -> p g i e", e=4),
             )
 
-        def quantize(name, src, w):
-            codes = keep.tile([P, w], U32, name=f"codes_{name}", align_bytes=64)
-            scales = keep.tile([P, w], U8, name=f"scales_{name}", align_bytes=64)
-            nc.vector.quantize_mx(out=codes[:].bitcast(FP8X4), scales=scales[:], in_=src)
+        def quantize(name, packed, width):
+            codes = keep.tile([P, width], U32, name=f"codes_{name}", align_bytes=64)
+            scales = keep.tile([P, width], U8, name=f"scales_{name}", align_bytes=64)
+            nc.vector.quantize_mx(out=codes[:].bitcast(FP8X4), scales=scales[:], in_=packed)
             return codes, scales
 
         picked = {}
-        packed = {}
-        for a in range(2):
-            for h in range(2):
-                picked[a, h] = keep.tile([P, PACK, H], F32, name=f"picked{a}{h}")
-                packed[a, h] = keep.tile([P, H * PACK], BF16, name=f"packed{a}{h}", align_bytes=64)
+        x_packed = {}
+        x_packed0 = keep.tile([P, S * PACK], BF16, name="x_packed0", align_bytes=64)
+        for half in range(2):
+            for a in range(PASSES):
+                picked[a, half] = keep.tile([P, PACK, HALF], F32, name=f"picked{a}{half}")
+            x_packed[0, half] = x_packed0[:, half * HALF * PACK : (half + 1) * HALF * PACK]
+            x_packed1 = keep.tile([P, HALF * PACK], BF16, name=f"x_packed1{half}", align_bytes=64)
+            x_packed[1, half] = x_packed1[:]
 
-        def gather(a, i, h, j0=0, w=H):
-            k0 = (h * H + j0) // 16
+        def pick(a, i, half, j0=0, width=HALF):
+            first = (half * HALF + j0) // LISTED
             nc.vector.tensor_tensor(
-                picked[a, h][:, i, j0 : j0 + w],
-                planes[a, i][:].indirect(offsets[:, k0 : k0 + w // 16]),
-                wg[h][:, j0 : j0 + w],
-                mult,
+                picked[a, half][:, i, j0 : j0 + width],
+                planes[a, i][:].indirect(offsets[:, first : first + width // LISTED]),
+                weights[half][:, j0 : j0 + width],
+                mybir.AluOpType.mult,
             )
 
-        def inter_x(engine_copy, a, h, j0, w):
-            interleave(engine_copy, packed[a, h][:, j0 * 4 : (j0 + w) * 4], picked[a, h][:, :, j0 : j0 + w])
+        def interleave_x(engine_copy, a, half, j0, width):
+            interleave(
+                engine_copy,
+                x_packed[a, half][:, j0 * PACK : (j0 + width) * PACK],
+                picked[a, half][:, :, j0 : j0 + width],
+            )
 
-        act, dve = nc.scalar.copy, nc.vector.tensor_copy
-        xq = {}
-        cq = {}
+        on_scalar, on_vector = nc.scalar.copy, nc.vector.tensor_copy
+        x_quantized = {}
+        c_quantized = {}
         c_packed = {}
-        for j0, w in ((0, 512), (512, 512)):
-            c_packed[j0] = keep.tile([P, w * PACK], BF16, name=f"c_packed{j0}", align_bytes=64)
+        for half in range(2):
+            c_packed[half] = keep.tile([P, HALF * PACK], BF16, name=f"c_packed{half}", align_bytes=64)
         u_packed = keep.tile([P, M * PACK], BF16, name="u_packed", align_bytes=64)
+        first_quarter = slice(0, QUARTER * PACK)
+        second_quarter = slice(QUARTER * PACK, HALF * PACK)
 
         for i in range(PACK):
-            gather(0, i, 0)
-            gather(0, i, 1)
-        inter_x(act, 0, 0, 0, H)
-        inter_x(act, 0, 1, 0, H)
-        for i in range(3):
-            gather(1, i, 0)
-            gather(1, i, 1)
-        interleave(act, u_packed[:], u_raw[:])
-        interleave(act, c_packed[0][:], c_raw[0][:])
-        xq[0, 0] = quantize("x00", packed[0, 0][:], H)
-        xq[0, 1] = quantize("x01", packed[0, 1][:], H)
-        uq = quantize("u", u_packed[:], M)
-        gather(1, 3, 0, 0, 256)
-        inter_x(act, 1, 0, 0, 256)
-        gather(1, 3, 0, 256, 256)
-        inter_x(act, 1, 0, 256, 256)
-        gather(1, 3, 1)
-        inter_x(act, 1, 1, 0, 256)
-        cq[0] = quantize("c0", c_packed[0][:], 512)
-        inter_x(dve, 1, 1, 256, 256)
-        xq[1, 0] = quantize("x10", packed[1, 0][:], H)
-        xq[1, 1] = quantize("x11", packed[1, 1][:], H)
-        interleave(dve, c_packed[512][:, 0:1024], c_raw[512][:, :, 0:256])
-        interleave(act, c_packed[512][:, 1024:2048], c_raw[512][:, :, 256:512])
-        cq[1] = quantize("c1", c_packed[512][:], 512)
+            pick(0, i, 0)
+            pick(0, i, 1)
+        interleave_x(on_scalar, 0, 0, 0, HALF)
+        interleave_x(on_scalar, 0, 1, 0, HALF)
 
-        c_at = {t: divmod(128 * t, 512) for t in range(8)}
-        banks = {}
-        for t in range(8):
-            banks[t] = psum.tile([P, M], F32, name=f"bank{t}")
-            h, o = divmod(t, 4)
-            cols = slice(o * P, (o + 1) * P)
-            for a in range(2):
-                codes, scales = xq[a, h]
+        pick(1, 0, 0)
+        pick(1, 0, 1)
+        interleave(on_scalar, u_packed[:], u_raw[:])
+        interleave(on_scalar, c_packed[0][:, first_quarter], c_raw[0][:])
+        pick(1, 1, 1)
+        pick(1, 2, 1)
+        pick(1, 1, 0)
+        pick(1, 2, 0)
+        for j0 in (0, QUARTER):
+            pick(1, 3, 1, j0, QUARTER)
+            interleave_x(on_scalar, 1, 1, j0, QUARTER)
+        codes0, scales0 = quantize("x0", x_packed0[:], S)
+        for half in range(2):
+            places = slice(half * HALF, (half + 1) * HALF)
+            x_quantized[0, half] = (codes0[:, places], scales0[:, places])
+        u_codes, u_scales = quantize("u", u_packed[:], M)
+        interleave(on_scalar, c_packed[0][:, second_quarter], c_raw[QUARTER][:])
+        for j0 in (0, QUARTER):
+            pick(1, 3, 0, j0, QUARTER)
+
+        interleave_x(on_scalar, 1, 0, 0, QUARTER)
+        x_quantized[1, 1] = quantize("x11", x_packed[1, 1], HALF)
+        interleave_x(on_vector, 1, 0, QUARTER, QUARTER)
+        c_quantized[0] = quantize("c0", c_packed[0][:], HALF)
+        interleave(on_scalar, c_packed[1][:, first_quarter], c_raw[HALF][:, :, 0:QUARTER])
+        x_quantized[1, 0] = quantize("x10", x_packed[1, 0], HALF)
+        interleave(on_vector, c_packed[1][:, second_quarter], c_raw[HALF][:, :, QUARTER:HALF])
+        c_quantized[1] = quantize("c1", c_packed[1][:], HALF)
+
+        sums = {}
+        for t in range(TILES):
+            sums[t] = psum.tile([P, M], F32, name=f"sum{t}")
+            half, j0 = divmod(t * P, HALF)
+            places = slice(j0, j0 + P)
+            for a in range(PASSES):
+                codes, scales = x_quantized[a, half]
                 nc.tensor.matmul_mx(
-                    out=banks[t][:],
-                    lhsT=codes[:, cols].bitcast(FP8X4),
-                    lhsT_scale=scales[:, cols],
-                    rhs=w4w[:, a, :].bitcast(FP4X4),
-                    rhs_scale=w4s[:, a, :],
+                    out=sums[t][:],
+                    lhsT=codes[:, places].bitcast(FP8X4),
+                    lhsT_scale=scales[:, places],
+                    rhs=w4_w[:, a, :].bitcast(FP4X4),
+                    rhs_scale=w4_s[:, a, :],
                     start=(a == 0),
                     stop=False,
                 )
-            b, o = c_at[t]
-            codes, scales = cq[b]
-            cols = slice(o, o + P)
+            codes, scales = c_quantized[half]
             nc.tensor.matmul_mx(
-                out=banks[t][:],
-                lhsT=codes[:, cols].bitcast(FP8X4),
-                lhsT_scale=scales[:, cols],
-                rhs=uq[0][:].bitcast(FP8X4),
-                rhs_scale=uq[1][:],
+                out=sums[t][:],
+                lhsT=codes[:, places].bitcast(FP8X4),
+                lhsT_scale=scales[:, places],
+                rhs=u_codes[:].bitcast(FP8X4),
+                rhs_scale=u_scales[:],
                 start=False,
                 stop=True,
             )
-        out_hbm = out.rearrange("(r t p) n -> r p t n", t=2, p=P)
-        for r in range(4):
-            res = keep.tile([P, 2, M], F32, name=f"res{r}")
-            nc.scalar.copy(res[:, 0, :], banks[2 * r][:])
-            nc.vector.tensor_copy(res[:, 1, :], banks[2 * r + 1][:])
-            nc.sync.dma_start(out_hbm[r], res[:])
+
+        out_hbm = out.rearrange("(r two p) n -> r p two n", two=2, p=P)
+        for r in range(TILES // 2):
+            result = keep.tile([P, 2, M], F32, name=f"result{r}")
+            nc.scalar.copy(result[:, 0, :], sums[2 * r][:])
+            nc.vector.tensor_copy(result[:, 1, :], sums[2 * r + 1][:])
+            nc.sync.dma_start(out_hbm[r], result[:])

from contextlib import ExitStack

import concourse.mybir as mybir

K, L, M, T, S = 1024, 512, 128, 2048, 1024
FLOPS = 2 * (K + L) * M * S

F32 = mybir.dt.float32
BF16 = mybir.dt.bfloat16
U32 = mybir.dt.uint32
I32 = mybir.dt.int32
U16 = mybir.dt.uint16
U8 = mybir.dt.uint8
FP8X4 = mybir.dt.float8_e4m3fn_x4
FP4X4 = mybir.dt.float4_e2m1fn_x4

P = 128
PACK = 4
PASSES = K // (P * PACK)
LISTED = 16
HALF = S // 2
QUARTER = S // 4
TILES = S // P
QUADRANT = 32
SCALE_ROWS = 4


def tile_list_hmix_tm_none_kernel(tc, xT, w4_words, w4_scales, c, u, wgt, offs, out):
    nc = tc.nc
    with ExitStack() as ctx:
        keep = ctx.enter_context(tc.tile_pool(name="keep", bufs=1))
        psum = ctx.enter_context(tc.psum_pool(name="psum", bufs=1))

        offsets = keep.tile([P, S // LISTED], U16, name="offsets")
        nc.sync.dma_start(offsets[:], offs)

        w4_w = keep.tile([P, PASSES, 2 * M], U8, name="w4_w", align_bytes=64)
        w4_s = keep.tile([P, PASSES, M], U8, name="w4_s", align_bytes=64)
        nc.gpsimd.memset(w4_s[:].bitcast(I32), 0)

        planes_hbm = xT.rearrange("(a p i) t -> a i p t", a=PASSES, i=PACK)
        planes = {}

        def load_plane(a, i):
            planes[a, i] = keep.tile([P, T], F32, name=f"plane{a}{i}")
            nc.sync.dma_start(planes[a, i][:], planes_hbm[a, i])

        c_hbm = c.rearrange("(p i) j -> p i j", i=PACK)
        c_raw = {}

        def load_c(j0, width):
            c_raw[j0] = keep.tile([P, PACK, width], F32, name=f"c_raw{j0}")
            nc.sync.dma_start(c_raw[j0][:], c_hbm[:, :, j0 : j0 + width])

        load_plane(0, 0)
        weights = {}
        for half in range(2):
            weights[half] = keep.tile([P, HALF], F32, name=f"wgt{half}")
            nc.sync.dma_start(weights[half][:], wgt[:, half * HALF : (half + 1) * HALF])
        load_plane(0, 1)
        load_plane(0, 2)
        nc.sync.dma_start(w4_w[:].bitcast(I32), w4_words.bitcast(I32).rearrange("a p n -> p a n"))
        for q in range(P // QUADRANT):
            nc.sync.dma_start(
                w4_s[QUADRANT * q : QUADRANT * q + SCALE_ROWS, :, :].bitcast(I32),
                w4_scales.bitcast(I32)[:, SCALE_ROWS * q : SCALE_ROWS * (q + 1), :].rearrange("a r n -> r a n"),
            )
        load_plane(0, 3)
        load_plane(1, 0)
        load_plane(1, 1)
        u_raw = keep.tile([P, PACK, M], F32, name="u_raw")
        nc.sync.dma_start(u_raw[:], u.rearrange("(p i) n -> p i n", i=PACK))
        load_c(0, QUARTER)
        load_plane(1, 2)
        load_c(QUARTER, QUARTER)
        load_plane(1, 3)
        load_c(HALF, HALF)

        def interleave(engine_copy, packed, raw):
            engine_copy(
                packed.rearrange("p (g e i) -> p g i e", i=PACK, e=4),
                raw.rearrange("p i (g e) -> p g i e", e=4),
            )

        def quantize(name, packed, width):
            codes = keep.tile([P, width], U32, name=f"codes_{name}", align_bytes=64)
            scales = keep.tile([P, width], U8, name=f"scales_{name}", align_bytes=64)
            nc.vector.quantize_mx(out=codes[:].bitcast(FP8X4), scales=scales[:], in_=packed)
            return codes, scales

        picked = {}
        x_packed = {}
        x_packed0 = keep.tile([P, S * PACK], BF16, name="x_packed0", align_bytes=64)
        for half in range(2):
            for a in range(PASSES):
                picked[a, half] = keep.tile([P, PACK, HALF], F32, name=f"picked{a}{half}")
            x_packed[0, half] = x_packed0[:, half * HALF * PACK : (half + 1) * HALF * PACK]
            x_packed1 = keep.tile([P, HALF * PACK], BF16, name=f"x_packed1{half}", align_bytes=64)
            x_packed[1, half] = x_packed1[:]

        def pick(a, i, half, j0=0, width=HALF):
            first = (half * HALF + j0) // LISTED
            nc.vector.tensor_tensor(
                picked[a, half][:, i, j0 : j0 + width],
                planes[a, i][:].indirect(offsets[:, first : first + width // LISTED]),
                weights[half][:, j0 : j0 + width],
                mybir.AluOpType.mult,
            )

        def interleave_x(engine_copy, a, half, j0, width):
            interleave(
                engine_copy,
                x_packed[a, half][:, j0 * PACK : (j0 + width) * PACK],
                picked[a, half][:, :, j0 : j0 + width],
            )

        on_scalar, on_vector = nc.scalar.copy, nc.vector.tensor_copy
        x_quantized = {}
        c_quantized = {}
        c_packed = {}
        for half in range(2):
            c_packed[half] = keep.tile([P, HALF * PACK], BF16, name=f"c_packed{half}", align_bytes=64)
        u_packed = keep.tile([P, M * PACK], BF16, name="u_packed", align_bytes=64)
        first_quarter = slice(0, QUARTER * PACK)
        second_quarter = slice(QUARTER * PACK, HALF * PACK)

        for i in range(PACK):
            pick(0, i, 0)
            pick(0, i, 1)
        interleave_x(on_scalar, 0, 0, 0, HALF)
        interleave_x(on_scalar, 0, 1, 0, HALF)

        pick(1, 0, 0)
        pick(1, 0, 1)
        interleave(on_scalar, u_packed[:], u_raw[:])
        interleave(on_scalar, c_packed[0][:, first_quarter], c_raw[0][:])
        pick(1, 1, 1)
        pick(1, 2, 1)
        pick(1, 1, 0)
        pick(1, 2, 0)
        for j0 in (0, QUARTER):
            pick(1, 3, 1, j0, QUARTER)
            interleave_x(on_scalar, 1, 1, j0, QUARTER)
        codes0, scales0 = quantize("x0", x_packed0[:], S)
        for half in range(2):
            places = slice(half * HALF, (half + 1) * HALF)
            x_quantized[0, half] = (codes0[:, places], scales0[:, places])
        u_codes, u_scales = quantize("u", u_packed[:], M)
        interleave(on_scalar, c_packed[0][:, second_quarter], c_raw[QUARTER][:])
        for j0 in (0, QUARTER):
            pick(1, 3, 0, j0, QUARTER)

        interleave_x(on_scalar, 1, 0, 0, QUARTER)
        x_quantized[1, 1] = quantize("x11", x_packed[1, 1], HALF)
        interleave_x(on_vector, 1, 0, QUARTER, QUARTER)
        c_quantized[0] = quantize("c0", c_packed[0][:], HALF)
        interleave(on_scalar, c_packed[1][:, first_quarter], c_raw[HALF][:, :, 0:QUARTER])
        x_quantized[1, 0] = quantize("x10", x_packed[1, 0], HALF)
        interleave(on_vector, c_packed[1][:, second_quarter], c_raw[HALF][:, :, QUARTER:HALF])
        c_quantized[1] = quantize("c1", c_packed[1][:], HALF)

        sums = {}
        for t in range(TILES):
            sums[t] = psum.tile([P, M], F32, name=f"sum{t}")
            half, j0 = divmod(t * P, HALF)
            places = slice(j0, j0 + P)
            for a in range(PASSES):
                codes, scales = x_quantized[a, half]
                nc.tensor.matmul_mx(
                    out=sums[t][:],
                    lhsT=codes[:, places].bitcast(FP8X4),
                    lhsT_scale=scales[:, places],
                    rhs=w4_w[:, a, :].bitcast(FP4X4),
                    rhs_scale=w4_s[:, a, :],
                    start=(a == 0),
                    stop=False,
                )
            codes, scales = c_quantized[half]
            nc.tensor.matmul_mx(
                out=sums[t][:],
                lhsT=codes[:, places].bitcast(FP8X4),
                lhsT_scale=scales[:, places],
                rhs=u_codes[:].bitcast(FP8X4),
                rhs_scale=u_scales[:],
                start=False,
                stop=True,
            )

        out_hbm = out.rearrange("(r two p) n -> r p two n", two=2, p=P)
        for r in range(TILES // 2):
            result = keep.tile([P, 2, M], F32, name=f"result{r}")
            nc.scalar.copy(result[:, 0, :], sums[2 * r][:])
            nc.vector.tensor_copy(result[:, 1, :], sums[2 * r + 1][:])
            nc.sync.dma_start(out_hbm[r], result[:])
